import numpy as np
import ml_dtypes


def mxq(x, axis, fmt="e4m3"):
    dtype, down = {"e4m3": (ml_dtypes.float8_e4m3fn, 7), "e5m2": (ml_dtypes.float8_e5m2, 14)}[fmt]
    v = np.moveaxis(np.asarray(x, np.float32).astype(ml_dtypes.bfloat16).astype(np.float64), axis, -1)
    blocks = v.reshape(v.shape[:-1] + (-1, 32))
    amax = np.abs(blocks).max(-1, keepdims=True)
    byte = np.maximum(np.where(amax > 0, np.frexp(amax)[1] - 1 + 127, 0) - down, 1)
    scale = np.exp2(byte - 127.0)
    codes = (blocks / scale).astype(np.float32).astype(dtype).astype(np.float64)
    return np.moveaxis((codes * scale).reshape(v.shape), -1, axis)


WIDE = False


def mx_kscale(k):
    if not WIDE:
        return np.ones(k)
    levels = np.array([10, -10, 5, -5, 0])
    if k % 512:
        return np.exp2(np.random.permutation(np.resize(levels, k // 32))).repeat(32)
    a = np.empty((k // 512, 16))
    for p in range(k // 512):
        a[p, :8] = np.random.permutation(np.resize(levels, 8))
        for g in range(8):
            far = levels[np.abs(levels - a[p, g]) >= 10]
            a[p, g + 8] = far[np.random.randint(len(far))]
    return np.exp2(a.ravel()).repeat(32)


def f64(x):
    return np.asarray(x).astype(np.float64)


def striped(idx):
    return np.tile(idx.reshape(-1, 16).T, (8, 1)).astype(np.uint16)


def unstriped(offs):
    return offs[:16].T.reshape(-1).astype(np.int64)


E2M1 = np.array([0.0, 0.5, 1.0, 1.5, 2.0, 3.0, 4.0, 6.0, -0.0, -0.5, -1.0, -1.5, -2.0, -3.0, -4.0, -6.0])


def pack_weight(w, fmt):
    k, n = w.shape
    w = f64(np.asarray(w, np.float32).astype(ml_dtypes.bfloat16)).reshape(k // 32, 32, n)
    amax = np.abs(w).max(1)
    if fmt == "e4m3":
        byte = np.frexp(amax)[1] - 1 + 127 - 7
    else:
        mant, ex = np.frexp(amax / 6.0)
        byte = np.where(mant > 0.5, ex, ex - 1) + 127
    byte = np.clip(np.where(amax > 0, byte, 1), 1, 254)
    scaled = (w * np.exp2(127.0 - byte)[:, None, :]).reshape(k, n).astype(np.float32)
    by_word = np.ascontiguousarray(scaled.reshape(k // 512, 128, 4, n).transpose(0, 1, 3, 2))
    if fmt == "e4m3":
        words = by_word.astype(ml_dtypes.float8_e4m3fn).view(np.uint8)
    else:
        c = by_word.astype(ml_dtypes.float4_e2m1fn).view(np.uint8) & 0xF
        words = (c[..., 0::2] | (c[..., 1::2] << 4)).reshape(k // 512, 128, 2 * n)
    return np.ascontiguousarray(words), np.ascontiguousarray(byte.astype(np.uint8).reshape(k // 512, 16, n))


def unpack_weight(words, scales, fmt):
    g, _, n = scales.shape
    words = np.ascontiguousarray(words).reshape(g, 128, n, -1)
    if fmt == "e4m3":
        vals = words.view(ml_dtypes.float8_e4m3fn).astype(np.float64)
    else:
        nib = np.empty((g, 128, n, 4), np.uint8)
        nib[..., 0::2] = words & 0xF
        nib[..., 1::2] = words >> 4
        vals = E2M1[nib]
    vals = vals * np.repeat(np.exp2(scales.astype(np.float64) - 127.0), 8, axis=1)[..., None]
    return vals.transpose(0, 1, 3, 2).reshape(g * 512, n)


def gelu(v):
    return 0.5 * v * (1.0 + np.tanh(np.sqrt(2.0 / np.pi) * (v + 0.044715 * v**3)))


T, S, K, H, N, T2, P = 4096, 1024, 512, 1024, 768, 2048, 1024

def setup_inputs():
    n = np.random.standard_normal
    s = mx_kscale(K)[:, None]
    u = mx_kscale(H)[:, None]
    d = {}
    d["tab_words"], d["tab_scales"] = pack_weight(n((K, T)) * s, "e4m3")
    d["offs"] = striped(np.random.permutation(T)[:S])
    d["w1"] = (1.5 * n((K, H)) / K**0.5 / s).astype(np.float32)
    d["w2_words"], d["w2_scales"] = pack_weight(n((K, H)) / K**0.5 / s, "e2m1")
    d["gain"] = (1.3 * np.exp(0.4 * n(H)) * u[:, 0]).astype(np.float32)
    d["page0"] = (n((H, T2)) * u).astype(np.float32)
    d["wgs"] = np.exp(0.3 * n((128, S))).astype(np.float32)
    d["offs2"] = striped(np.random.permutation(T2)[:S])
    d["offs3"] = striped(np.random.permutation(T2)[:P])
    d["w3"] = (1.2 * n((H, N)) / H**0.5 / u).astype(np.float32)
    d["page1"] = n((N, T2)).astype(np.float32)
    d["wgo"] = np.exp(0.3 * n((128, P))).astype(np.float32)
    d["offs4"] = striped(np.random.permutation(T2)[:P])
    return d

def reference(tab_words, tab_scales, offs, w1, w2_words, w2_scales, gain, page0, wgs, offs2, offs3, w3, page1, wgo, offs4):
    v = unpack_weight(tab_words, tab_scales, "e4m3")[:, unstriped(offs)]
    a = mxq(f64(w1), 0, "e4m3").T @ v
    b = unpack_weight(w2_words, w2_scales, "e2m1").T @ v
    gap = np.tanh(a) - b
    h = a / (1.0 + np.square(gap)) * f64(gain)[:, None]
    page = f64(page0).copy()
    page[:, unstriped(offs2)] = np.tile(f64(wgs), (H // 128, 1)) * h
    x = mxq(page[:, unstriped(offs3)], 0, "e4m3")
    y = np.abs(mxq(f64(w3), 0, "e4m3").T @ x)
    out = f64(page1).copy()
    out[:, unstriped(offs4)] = np.tile(f64(wgo), (N // 128, 1)) * y
    return out

@@ -1,0 +1,302 @@
+from contextlib import ExitStack
+
+import concourse.mybir as mybir
+from concourse.masks import make_identity
+
+T, S, K, H, N, T2, M = 4096, 1024, 512, 1024, 768, 2048, 1024
+FLOPS = 2 * (2 * K * H * S + H * N * M)
+
+F32 = mybir.dt.float32
+BF16 = mybir.dt.bfloat16
+I32 = mybir.dt.int32
+U32 = mybir.dt.uint32
+U16 = mybir.dt.uint16
+U8 = mybir.dt.uint8
+FP8X4 = mybir.dt.float8_e4m3fn_x4
+FP4X4 = mybir.dt.float4_e2m1fn_x4
+ACT = mybir.ActivationFunctionType
+MULT = mybir.AluOpType.mult
+ADD = mybir.AluOpType.add
+
+P = 128
+PACK = 4
+HALF = 512
+LIST_HALF = HALF // 16
+PASSES = H // (P * PACK)
+SLICES = H // P
+OUT_SLICES = N // P
+
+
+def tile_list_sewer_defect_recall_kernel(
+    tc, tab_words, tab_scales, offs, w1, w2_words, w2_scales, gain, page0, wgs, offs2, offs3, w3, page1, wgo, offs4, out
+):
+    nc = tc.nc
+    with ExitStack() as ctx:
+        keep = ctx.enter_context(tc.tile_pool(name="keep", bufs=1))
+        work = ctx.enter_context(tc.tile_pool(name="work", bufs=1))
+        psum = ctx.enter_context(tc.psum_pool(name="psum", bufs=1))
+
+        def half(h):
+            return slice(h * HALF, (h + 1) * HALF)
+
+        def list_half(h):
+            return slice(h * LIST_HALF, (h + 1) * LIST_HALF)
+
+        def load_list(src, name):
+            tile = keep.tile([P, S // 16], U16, name=name)
+            nc.sync.dma_start(tile[:], src)
+            return tile
+
+        def load_scale_rows(queue, tile, src):
+            for q in range(4):
+                queue.dma_start(tile[32 * q : 32 * q + 4, :].bitcast(I32), src[0, 4 * q : 4 * q + 4, :].bitcast(I32))
+
+        def load_w1(g, tag, parts):
+            raw = work.tile([P, PACK, HALF], F32, tag=tag, align_bytes=64, name="w1_raw")
+            rows = w1[:, half(g)].rearrange("(p j) c -> p j c", j=PACK)
+            for j in range(0, PACK, PACK // parts):
+                nc.sync.dma_start(raw[:, j : j + PACK // parts, :], rows[:, j : j + PACK // parts, :])
+            return raw
+
+        def load_w3(g):
+            raw = work.tile([P, PACK, N], F32, tag=("raw_a", "raw_b")[g], align_bytes=64, name="w3_raw")
+            nc.sync.dma_start(raw[:], w3[half(g), :].rearrange("(p j) c -> p j c", j=PACK))
+            return raw
+
+        def load_wgs(pair):
+            tile = work.tile([P, 2, S], F32, tag="wgs%d" % pair, name="wgs_rows")
+            rows = wgs.rearrange("(q t) j -> q t j", t=PACK)[:, 2 * pair : 2 * pair + 2, :]
+            for q in range(4):
+                nc.sync.dma_start(tile[32 * q : 32 * q + 32, :, :], rows)
+            return tile
+
+        def load_page0(s):
+            g, t = divmod(s, PACK)
+            tile = work.tile([P, T2], F32, tag="page0", bufs=6, name="page0_rows")
+            nc.sync.dma_start(tile[:], page0[half(g), :].rearrange("(p t) c -> t p c", t=PACK)[t])
+            return tile
+
+        def load_page1(n):
+            if n < 4:
+                tile = work.tile([P, T2], F32, tag="page1", bufs=4, name="page1_rows")
+            else:
+                tile = work.tile([P, T2], F32, tag="page0", bufs=6, name="page1_rows")
+            nc.sync.dma_start(tile[:], page1[n * P : (n + 1) * P, :])
+            return tile
+
+        tab_sc = work.tile([P, T], U8, tag="tabsc", align_bytes=64, name="tab_sc")
+        nc.vector.memset(tab_sc[:].bitcast(I32), 0)
+        w2_sc_raw = keep.tile([P, H], U8, name="w2_sc_raw")
+        nc.vector.memset(w2_sc_raw[:].bitcast(I32), 0)
+        ident = keep.tile([P, P], F32, name="ident")
+        make_identity(nc, ident[:])
+
+        list1 = load_list(offs, "list1")
+        list2 = load_list(offs2, "list2")
+        list3 = load_list(offs3, "list3")
+        list4 = load_list(offs4, "list4")
+        gains = keep.tile([P, PASSES, PACK], F32, name="gains")
+        nc.sync.dma_start(gains[:], gain.rearrange("(g p t) -> p g t", g=PASSES, t=PACK))
+        w2_raw = keep.tile([P, 2 * H], U8, name="w2_raw")
+        nc.sync.dma_start(w2_raw[:].bitcast(I32), w2_words[0].bitcast(I32))
+        w1_raw = [load_w1(0, "raw_a", 2)]
+        load_scale_rows(nc.sync, tab_sc, tab_scales)
+        tab_w = work.tile([P, T], U32, tag="raw_b", align_bytes=64, name="tab_w")
+        nc.sync.dma_start(tab_w[:].bitcast(I32), tab_words[0].rearrange("p n t -> p (n t)").bitcast(I32))
+        load_scale_rows(nc.sync, w2_sc_raw, w2_scales)
+        w1_raw.append(load_w1(1, "raw_c", 1))
+        wgs_rows = [load_wgs(0)]
+        pages0 = [load_page0(0)]
+
+        w1_codes = []
+        w1_sc = [keep.tile([P, HALF], U8, align_bytes=64, name="w1_sc%d" % g) for g in range(PASSES)]
+        w2_codes = [keep.tile([P, 2 * HALF], U8, align_bytes=64, name="w2_codes%d" % g) for g in range(PASSES)]
+        w2_sc = []
+
+        def staging(tag, width=PACK * HALF):
+            return work.tile([P, width], BF16, tag=tag, align_bytes=64, name="staging")
+
+        def prepare_w1(g):
+            grouped = staging(("stage0", "raw_b")[g])
+            dst = grouped[:].rearrange("p (t m j) -> p m t j", t=PACK, j=PACK)
+            src = w1_raw[g][:].rearrange("p j (m t) -> p m t j", t=PACK)
+            if g == 0:
+                nc.scalar.copy(dst, src)
+            else:
+                nc.vector.tensor_copy(dst, src)
+            w1_codes.append(work.tile([P, HALF], U32, tag=("tabsc", "w1_second")[g], align_bytes=64, name="w1_codes"))
+            nc.vector.quantize_mx(out=w1_codes[g][:].bitcast(FP8X4), scales=w1_sc[g][:], in_=grouped[:])
+
+        def deal_w2_codes(g):
+            nc.vector.tensor_copy(
+                w2_codes[g][:].rearrange("p (t m b) -> p t m b", t=PACK, b=2),
+                w2_raw[:, 2 * HALF * g : 2 * HALF * (g + 1)].rearrange("p (m t b) -> p t m b", t=PACK, b=2),
+            )
+
+        def deal_w2_scales(g):
+            w2_sc.append(work.tile([P, HALF], U8, tag=("w2_first", "raw_c")[g], align_bytes=64, name="w2_sc"))
+            nc.vector.tensor_copy(
+                w2_sc[g][:].rearrange("p (t m) -> p t m", t=PACK),
+                w2_sc_raw[:, half(g)].rearrange("p (m t) -> p t m", t=PACK),
+            )
+
+        v_sc = keep.tile([P, S], U8, align_bytes=64, name="v_sc")
+        v_codes = [keep.tile([P, HALF], U32, align_bytes=64, name="v_codes%d" % h) for h in range(2)]
+        for g in range(PASSES):
+            deal_w2_codes(g)
+        nc.vector.tensor_copy(v_sc[:], tab_sc[:].indirect(list1[:]))
+        prepare_w1(0)
+        nc.vector.tensor_copy(v_codes[0][:], tab_w[:].indirect(list1[:, list_half(0)]))
+        deal_w2_scales(0)
+        nc.vector.tensor_copy(v_codes[1][:], tab_w[:].indirect(list1[:, list_half(1)]))
+        prepare_w1(1)
+        deal_w2_scales(1)
+        pages0.append(load_page0(1))
+        wgs_rows.append(load_wgs(1))
+        for s in range(2, 6):
+            pages0.append(load_page0(s))
+        pages1 = [load_page1(n) for n in range(4)]
+        w3_raw = [load_w3(g) for g in range(PASSES)]
+
+        w3_codes = [keep.tile([P, N], U32, align_bytes=64, name="w3_codes%d" % g) for g in range(PASSES)]
+        w3_sc = [keep.tile([P, N], U8, align_bytes=64, name="w3_sc%d" % g) for g in range(PASSES)]
+        x_codes = [keep.tile([P, M], U32, align_bytes=64, name="x_codes%d" % g) for g in range(PASSES)]
+        x_sc = [keep.tile([P, M], U8, align_bytes=64, name="x_sc%d" % g) for g in range(PASSES)]
+
+        def interleave(grouped, planes, c0, width, step=64):
+            dst = grouped.rearrange("p (c i t) -> p c t i", i=4, t=PACK)
+            src = planes[:, :, c0 : c0 + width].rearrange("p t (c i) -> p c t i", i=4)
+            for b in range(0, width // 4, step):
+                nc.scalar.copy(dst[:, b : b + step], src[:, b : b + step])
+
+        picked = {}
+
+        def gather_x(s, h):
+            g, t = divmod(s, PACK)
+            if t == 0:
+                tag = {(0, 0): "x00", (0, 1): "x01", (1, 0): "x10", (1, 1): "stage0"}[g, h]
+                picked[g, h] = work.tile([P, PACK, HALF], BF16, tag=tag, align_bytes=64, name="picked")
+            nc.vector.tensor_copy(picked[g, h][:, t, :], pages0[s][:].indirect(list3[:, list_half(h)]))
+
+        def prepare_w3_and_first_pass():
+            grouped = staging("tanh_root", PACK * (PASSES * N + M))
+            for g in range(PASSES):
+                interleave(grouped[:, PACK * N * g : PACK * N * (g + 1)], w3_raw[g], 0, N)
+            x_at = PACK * N * PASSES
+            for h in range(2):
+                interleave(grouped[:, x_at + PACK * HALF * h : x_at + PACK * HALF * (h + 1)], picked[0, h], 0, HALF)
+            for g in range(PASSES):
+                for c0, c1 in ((0, HALF), (HALF, N)):
+                    nc.vector.quantize_mx(
+                        out=w3_codes[g][:, c0:c1].bitcast(FP8X4),
+                        scales=w3_sc[g][:, c0:c1],
+                        in_=grouped[:, PACK * (N * g + c0) : PACK * (N * g + c1)],
+                    )
+            nc.vector.quantize_mx(out=x_codes[0][:].bitcast(FP8X4), scales=x_sc[0][:], in_=grouped[:, x_at:])
+
+        def prepare_x_second_pass(h):
+            grouped = staging(("stage0", "x10")[h])
+            interleave(grouped[:], picked[1, h], 0, HALF, 32)
+            nc.vector.quantize_mx(out=x_codes[1][:, half(h)].bitcast(FP8X4), scales=x_sc[1][:, half(h)], in_=grouped[:])
+
+        def bank(index, name):
+            return psum.tile([P, HALF], F32, tag="bank%d" % index, name=name)
+
+        def stage_one(batch, slices):
+            on_vector = batch == 0
+            product_banks, turn_banks = 4 * (batch % 2), 4 * (1 - batch % 2)
+            units = [(s, h) for s in slices for h in range(2)]
+            neg_tanh = work.tile([P, len(units), HALF], F32, tag="tanh_root", align_bytes=64, name="neg_tanh")
+            scaled = {s: work.tile([P, S], F32, tag="aw%d" % (0 if s == 0 else (s + 1) % 2), align_bytes=64, name="scaled") for s in slices}
+            a_banks, back_banks = [], []
+            for u, (s, h) in enumerate(units):
+                g, t = divmod(s, PACK)
+                cols = slice(t * P, (t + 1) * P)
+                b = bank(product_banks + u, "b")
+                nc.tensor.matmul_mx(
+                    out=b[:], lhsT=w2_codes[g][:, 2 * t * P : 2 * (t + 1) * P].bitcast(FP4X4), lhsT_scale=w2_sc[g][:, cols],
+                    rhs=v_codes[h][:].bitcast(FP8X4), rhs_scale=v_sc[:, half(h)], start=True, stop=True,
+                )
+                b_sb = work.tile([P, HALF], F32, tag="b_sb", bufs=2, name="b_sb")
+                if not on_vector:
+                    nc.scalar.copy(b_sb[:], b[:])
+                a = bank(product_banks + (u + len(units)) % 4, "a")
+                nc.tensor.matmul_mx(
+                    out=a[:], lhsT=w1_codes[g][:, cols].bitcast(FP8X4), lhsT_scale=w1_sc[g][:, cols],
+                    rhs=v_codes[h][:].bitcast(FP8X4), rhs_scale=v_sc[:, half(h)], start=True, stop=True,
+                )
+                nc.scalar.activation(neg_tanh[:, u, :], a[:], ACT.Tanh, scale=-1.0)
+                gap_sq = work.tile([P, HALF], F32, tag="gap_sq", bufs=4, name="gap_sq")
+                if on_vector:
+                    nc.vector.tensor_tensor(b_sb[:], b[:], neg_tanh[:, u, :], ADD)
+                    nc.vector.tensor_tensor(gap_sq[:], b_sb[:], b_sb[:], MULT)
+                else:
+                    gap = bank(turn_banks + u, "gap")
+                    for c in range(4):
+                        blk = slice(c * P, (c + 1) * P)
+                        nc.tensor.matmul(gap[:, blk], neg_tanh[:, u, blk], ident[:], start=True, stop=False, is_transpose=True)
+                        nc.tensor.matmul(gap[:, blk], b_sb[:, blk], ident[:], start=False, stop=True, is_transpose=True)
+                    nc.scalar.activation(gap_sq[:], gap[:], ACT.Square)
+                a_banks.append(a)
+                back_banks.append(gap_sq)
+            for u, (s, h) in enumerate(units):
+                g, t = divmod(s, PACK)
+                nc.vector.scalar_tensor_tensor(
+                    scaled[s][:, half(h)], a_banks[u][:], gains[:, g, t : t + 1], wgs_rows[t // 2][:, t % 2, half(h)], MULT, MULT
+                )
+            root = work.tile([P, len(units), HALF], F32, tag="tanh_root", align_bytes=64, name="root")
+            damp = {s: work.tile([P, S], F32, tag="damp", bufs=3, name="damp") for s in slices}
+            for u, (s, h) in enumerate(units):
+                if on_vector:
+                    back = back_banks[u]
+                else:
+                    back = bank(turn_banks + u, "back")
+                    for c in range(4):
+                        blk = slice(c * P, (c + 1) * P)
+                        nc.tensor.transpose(back[:, blk], back_banks[u][:, blk], ident[:])
+                nc.scalar.activation(root[:, u, :], back[:], ACT.Abs_reciprocal_sqrt, bias=1.0)
+                nc.scalar.activation(damp[s][:, half(h)], root[:, u, :], ACT.Square)
+            for s in slices:
+                nc.vector.tensor_tensor(pages0[s][:].indirect(list2[:]), damp[s][:], scaled[s][:], MULT)
+                gather_x(s, 0)
+                if s < PACK:
+                    gather_x(s, 1)
+
+        stage_one(0, (0,))
+        pages0.append(load_page0(6))
+        stage_one(1, (1,))
+        pages0.append(load_page0(7))
+        stage_one(2, (2, 3))
+        stage_one(3, (4, 5))
+        wgo_rows = work.tile([P, M], F32, tag="wgs0", name="wgo_rows")
+        nc.sync.dma_start(wgo_rows[:], wgo)
+        pages1.extend(load_page1(n) for n in range(4, OUT_SLICES))
+        stage_one(4, (6, 7))
+        prepare_w3_and_first_pass()
+        prepare_x_second_pass(0)
+        for s in range(PACK, SLICES):
+            gather_x(s, 1)
+
+        def stage_two(n, h):
+            cols = slice(n * P, (n + 1) * P)
+            y = bank((2 * n + h) % 8, "y")
+            for g in range(PASSES):
+                nc.tensor.matmul_mx(
+                    out=y[:], lhsT=w3_codes[g][:, cols].bitcast(FP8X4), lhsT_scale=w3_sc[g][:, cols],
+                    rhs=x_codes[g][:, half(h)].bitcast(FP8X4), rhs_scale=x_sc[g][:, half(h)], start=(g == 0), stop=(g == PASSES - 1),
+                )
+            size = work.tile([P, HALF], F32, tag="gap_sq", bufs=4, name="size")
+            nc.scalar.activation(size[:], y[:], ACT.Abs)
+            nc.vector.tensor_tensor(pages1[n][:].indirect(list4[:, list_half(h)]), size[:], wgo_rows[:, half(h)], MULT)
+            if h == 1:
+                nc.sync.dma_start(out[cols, :], pages1[n][:])
+
+        stage_two(0, 0)
+        prepare_x_second_pass(1)
+        stage_two(1, 0)
+        stage_two(2, 0)
+        for n in range(3):
+            stage_two(n, 1)
+        for n in range(3, OUT_SLICES):
+            stage_two(n, 0)
+            stage_two(n, 1)

@@ -104,7 +104,6 @@ def tile_list_sewer_defect_recall_kernel(
         tab_w = work.tile([P, T], U32, tag="raw_b", align_bytes=64, name="tab_w")
         nc.sync.dma_start(tab_w[:].bitcast(I32), tab_words[0].rearrange("p n t -> p (n t)").bitcast(I32))
         load_scale_rows(nc.sync, w2_sc_raw, w2_scales)
-        w1_raw.append(load_w1(1, "raw_c", 1))
         wgs_rows = [load_wgs(0)]
         pages0 = [load_page0(0)]
 
@@ -120,10 +119,9 @@ def tile_list_sewer_defect_recall_kernel(
             grouped = staging(("stage0", "raw_b")[g])
             dst = grouped[:].rearrange("p (t m j) -> p m t j", t=PACK, j=PACK)
             src = w1_raw[g][:].rearrange("p j (m t) -> p m t j", t=PACK)
-            if g == 0:
-                nc.scalar.copy(dst, src)
-            else:
-                nc.vector.tensor_copy(dst, src)
+            step = (P, 32)[g]
+            for m in range(0, P, step):
+                nc.scalar.copy(dst[:, m : m + step], src[:, m : m + step])
             w1_codes.append(work.tile([P, HALF], U32, tag=("tabsc", "w1_second")[g], align_bytes=64, name="w1_codes"))
             nc.vector.quantize_mx(out=w1_codes[g][:].bitcast(FP8X4), scales=w1_sc[g][:], in_=grouped[:])
 
@@ -149,14 +147,12 @@ def tile_list_sewer_defect_recall_kernel(
         nc.vector.tensor_copy(v_codes[0][:], tab_w[:].indirect(list1[:, list_half(0)]))
         deal_w2_scales(0)
         nc.vector.tensor_copy(v_codes[1][:], tab_w[:].indirect(list1[:, list_half(1)]))
-        prepare_w1(1)
-        deal_w2_scales(1)
         pages0.append(load_page0(1))
+        w1_raw.append(load_w1(1, "raw_c", 1))
         wgs_rows.append(load_wgs(1))
         for s in range(2, 6):
             pages0.append(load_page0(s))
         pages1 = [load_page1(n) for n in range(4)]
-        w3_raw = [load_w3(g) for g in range(PASSES)]
 
         w3_codes = [keep.tile([P, N], U32, align_bytes=64, name="w3_codes%d" % g) for g in range(PASSES)]
         w3_sc = [keep.tile([P, N], U8, align_bytes=64, name="w3_sc%d" % g) for g in range(PASSES)]
@@ -169,22 +165,23 @@ def tile_list_sewer_defect_recall_kernel(
             for b in range(0, width // 4, step):
                 nc.scalar.copy(dst[:, b : b + step], src[:, b : b + step])
 
-        picked = {}
+        picked_first = work.tile([P, PACK, M], BF16, tag="x0", align_bytes=64, name="picked_first")
+        picked_second = []
 
-        def gather_x(s, h):
-            g, t = divmod(s, PACK)
-            if t == 0:
-                tag = {(0, 0): "x00", (0, 1): "x01", (1, 0): "x10", (1, 1): "stage0"}[g, h]
-                picked[g, h] = work.tile([P, PACK, HALF], BF16, tag=tag, align_bytes=64, name="picked")
-            nc.vector.tensor_copy(picked[g, h][:, t, :], pages0[s][:].indirect(list3[:, list_half(h)]))
+        def gather_first_pass(s):
+            nc.vector.tensor_copy(picked_first[:, s, :], pages0[s][:].indirect(list3[:]))
+
+        def gather_second_pass(s, h):
+            if s == PACK:
+                picked_second.append(work.tile([P, PACK, HALF], BF16, tag=("x10", "stage0")[h], align_bytes=64, name="picked_second"))
+            nc.vector.tensor_copy(picked_second[h][:, s - PACK, :], pages0[s][:].indirect(list3[:, list_half(h)]))
 
         def prepare_w3_and_first_pass():
             grouped = staging("tanh_root", PACK * (PASSES * N + M))
             for g in range(PASSES):
                 interleave(grouped[:, PACK * N * g : PACK * N * (g + 1)], w3_raw[g], 0, N)
             x_at = PACK * N * PASSES
-            for h in range(2):
-                interleave(grouped[:, x_at + PACK * HALF * h : x_at + PACK * HALF * (h + 1)], picked[0, h], 0, HALF)
+            interleave(grouped[:, x_at:], picked_first, 0, M)
             for g in range(PASSES):
                 for c0, c1 in ((0, HALF), (HALF, N)):
                     nc.vector.quantize_mx(
@@ -196,36 +193,48 @@ def tile_list_sewer_defect_recall_kernel(
 
         def prepare_x_second_pass(h):
             grouped = staging(("stage0", "x10")[h])
-            interleave(grouped[:], picked[1, h], 0, HALF, 32)
+            interleave(grouped[:], picked_second[h], 0, HALF, 32)
             nc.vector.quantize_mx(out=x_codes[1][:, half(h)].bitcast(FP8X4), scales=x_sc[1][:, half(h)], in_=grouped[:])
 
         def bank(index, name):
             return psum.tile([P, HALF], F32, tag="bank%d" % index, name=name)
+
+        def features(index, s, h, neg_tanh):
+            g, t = divmod(s, PACK)
+            cols = slice(t * P, (t + 1) * P)
+            a = bank(index, "a")
+            nc.tensor.matmul_mx(
+                out=a[:], lhsT=w1_codes[g][:, cols].bitcast(FP8X4), lhsT_scale=w1_sc[g][:, cols],
+                rhs=v_codes[h][:].bitcast(FP8X4), rhs_scale=v_sc[:, half(h)], start=True, stop=True,
+            )
+            nc.scalar.activation(neg_tanh, a[:], ACT.Tanh, scale=-1.0)
+            return a
+
+        def codes(index, s, h):
+            g, t = divmod(s, PACK)
+            b = bank(index, "b")
+            nc.tensor.matmul_mx(
+                out=b[:], lhsT=w2_codes[g][:, 2 * t * P : 2 * (t + 1) * P].bitcast(FP4X4), lhsT_scale=w2_sc[g][:, t * P : (t + 1) * P],
+                rhs=v_codes[h][:].bitcast(FP8X4), rhs_scale=v_sc[:, half(h)], start=True, stop=True,
+            )
+            return b
 
         def stage_one(batch, slices):
             on_vector = batch == 0
             product_banks, turn_banks = 4 * (batch % 2), 4 * (1 - batch % 2)
             units = [(s, h) for s in slices for h in range(2)]
             neg_tanh = work.tile([P, len(units), HALF], F32, tag="tanh_root", align_bytes=64, name="neg_tanh")
-            scaled = {s: work.tile([P, S], F32, tag="aw%d" % (0 if s == 0 else (s + 1) % 2), align_bytes=64, name="scaled") for s in slices}
+            scaled = {s: work.tile([P, S], F32, tag="aw%d" % (s % 2), align_bytes=64, name="scaled") for s in slices}
             a_banks, back_banks = [], []
             for u, (s, h) in enumerate(units):
-                g, t = divmod(s, PACK)
-                cols = slice(t * P, (t + 1) * P)
-                b = bank(product_banks + u, "b")
-                nc.tensor.matmul_mx(
-                    out=b[:], lhsT=w2_codes[g][:, 2 * t * P : 2 * (t + 1) * P].bitcast(FP4X4), lhsT_scale=w2_sc[g][:, cols],
-                    rhs=v_codes[h][:].bitcast(FP8X4), rhs_scale=v_sc[:, half(h)], start=True, stop=True,
-                )
                 b_sb = work.tile([P, HALF], F32, tag="b_sb", bufs=2, name="b_sb")
-                if not on_vector:
+                if on_vector:
+                    a = features(product_banks + u, s, h, neg_tanh[:, u, :])
+                    b = codes(turn_banks + u, s, h)
+                else:
+                    b = codes(product_banks + u, s, h)
                     nc.scalar.copy(b_sb[:], b[:])
-                a = bank(product_banks + (u + len(units)) % 4, "a")
-                nc.tensor.matmul_mx(
-                    out=a[:], lhsT=w1_codes[g][:, cols].bitcast(FP8X4), lhsT_scale=w1_sc[g][:, cols],
-                    rhs=v_codes[h][:].bitcast(FP8X4), rhs_scale=v_sc[:, half(h)], start=True, stop=True,
-                )
-                nc.scalar.activation(neg_tanh[:, u, :], a[:], ACT.Tanh, scale=-1.0)
+                    a = features(product_banks + u, s, h, neg_tanh[:, u, :])
                 gap_sq = work.tile([P, HALF], F32, tag="gap_sq", bufs=4, name="gap_sq")
                 if on_vector:
                     nc.vector.tensor_tensor(b_sb[:], b[:], neg_tanh[:, u, :], ADD)
@@ -257,27 +266,36 @@ def tile_list_sewer_defect_recall_kernel(
                 nc.scalar.activation(root[:, u, :], back[:], ACT.Abs_reciprocal_sqrt, bias=1.0)
                 nc.scalar.activation(damp[s][:, half(h)], root[:, u, :], ACT.Square)
             for s in slices:
-                nc.vector.tensor_tensor(pages0[s][:].indirect(list2[:]), damp[s][:], scaled[s][:], MULT)
-                gather_x(s, 0)
+                if s == 0:
+                    for h in range(2):
+                        nc.vector.tensor_tensor(
+                            pages0[s][:].indirect(list2[:, list_half(h)]), damp[s][:, half(h)], scaled[s][:, half(h)], MULT
+                        )
+                else:
+                    nc.vector.tensor_tensor(pages0[s][:].indirect(list2[:]), damp[s][:], scaled[s][:], MULT)
                 if s < PACK:
-                    gather_x(s, 1)
+                    gather_first_pass(s)
+                else:
+                    gather_second_pass(s, 0)
 
-        stage_one(0, (0,))
+        stage_one(0, (0, 1))
+        prepare_w1(1)
+        deal_w2_scales(1)
         pages0.append(load_page0(6))
-        stage_one(1, (1,))
         pages0.append(load_page0(7))
-        stage_one(2, (2, 3))
-        stage_one(3, (4, 5))
+        w3_raw = [load_w3(g) for g in range(PASSES)]
+        stage_one(1, (2, 3))
+        stage_one(2, (4, 5))
         wgo_rows = work.tile([P, M], F32, tag="wgs0", name="wgo_rows")
         nc.sync.dma_start(wgo_rows[:], wgo)
         pages1.extend(load_page1(n) for n in range(4, OUT_SLICES))
-        stage_one(4, (6, 7))
+        stage_one(3, (6, 7))
         prepare_w3_and_first_pass()
         prepare_x_second_pass(0)
         for s in range(PACK, SLICES):
-            gather_x(s, 1)
+            gather_second_pass(s, 1)
 
-        def stage_two(n, h):
+        def scores(n, h, size):
             cols = slice(n * P, (n + 1) * P)
             y = bank((2 * n + h) % 8, "y")
             for g in range(PASSES):
@@ -285,18 +303,29 @@ def tile_list_sewer_defect_recall_kernel(
                     out=y[:], lhsT=w3_codes[g][:, cols].bitcast(FP8X4), lhsT_scale=w3_sc[g][:, cols],
                     rhs=x_codes[g][:, half(h)].bitcast(FP8X4), rhs_scale=x_sc[g][:, half(h)], start=(g == 0), stop=(g == PASSES - 1),
                 )
-            size = work.tile([P, HALF], F32, tag="gap_sq", bufs=4, name="size")
-            nc.scalar.activation(size[:], y[:], ACT.Abs)
-            nc.vector.tensor_tensor(pages1[n][:].indirect(list4[:, list_half(h)]), size[:], wgo_rows[:, half(h)], MULT)
-            if h == 1:
-                nc.sync.dma_start(out[cols, :], pages1[n][:])
+            nc.scalar.activation(size, y[:], ACT.Abs)
 
-        stage_two(0, 0)
+        def store(n):
+            nc.sync.dma_start(out[n * P : (n + 1) * P, :], pages1[n][:])
+
+        def put_half(n, h):
+            size = work.tile([P, HALF], F32, tag="gap_sq", bufs=4, name="size")
+            scores(n, h, size[:])
+            nc.vector.tensor_tensor(pages1[n][:].indirect(list4[:, list_half(h)]), size[:], wgo_rows[:, half(h)], MULT)
+
+        def put_whole(n):
+            size = work.tile([P, M], F32, tag="damp", bufs=3, name="size")
+            for h in range(2):
+                scores(n, h, size[:, half(h)])
+            nc.vector.tensor_tensor(pages1[n][:].indirect(list4[:]), size[:], wgo_rows[:], MULT)
+
+        put_half(0, 0)
         prepare_x_second_pass(1)
-        stage_two(1, 0)
-        stage_two(2, 0)
+        put_half(1, 0)
+        put_half(2, 0)
         for n in range(3):
-            stage_two(n, 1)
+            put_half(n, 1)
+            store(n)
         for n in range(3, OUT_SLICES):
-            stage_two(n, 0)
-            stage_two(n, 1)
+            put_whole(n)
+            store(n)

@@ -104,6 +104,7 @@ def tile_list_sewer_defect_recall_kernel(
         tab_w = work.tile([P, T], U32, tag="raw_b", align_bytes=64, name="tab_w")
         nc.sync.dma_start(tab_w[:].bitcast(I32), tab_words[0].rearrange("p n t -> p (n t)").bitcast(I32))
         load_scale_rows(nc.sync, w2_sc_raw, w2_scales)
+        w1_raw.append(load_w1(1, "raw_c", 1))
         wgs_rows = [load_wgs(0)]
         pages0 = [load_page0(0)]
 
@@ -119,9 +120,11 @@ def tile_list_sewer_defect_recall_kernel(
             grouped = staging(("stage0", "raw_b")[g])
             dst = grouped[:].rearrange("p (t m j) -> p m t j", t=PACK, j=PACK)
             src = w1_raw[g][:].rearrange("p j (m t) -> p m t j", t=PACK)
-            step = (P, 32)[g]
-            for m in range(0, P, step):
-                nc.scalar.copy(dst[:, m : m + step], src[:, m : m + step])
+            if g == 0:
+                nc.scalar.copy(dst, src)
+            else:
+                for m in range(0, P, 32):
+                    nc.gpsimd.tensor_scalar(dst[:, m : m + 32], src[:, m : m + 32], 1.0, 0.0, MULT, ADD)
             w1_codes.append(work.tile([P, HALF], U32, tag=("tabsc", "w1_second")[g], align_bytes=64, name="w1_codes"))
             nc.vector.quantize_mx(out=w1_codes[g][:].bitcast(FP8X4), scales=w1_sc[g][:], in_=grouped[:])
 
@@ -148,7 +151,6 @@ def tile_list_sewer_defect_recall_kernel(
         deal_w2_scales(0)
         nc.vector.tensor_copy(v_codes[1][:], tab_w[:].indirect(list1[:, list_half(1)]))
         pages0.append(load_page0(1))
-        w1_raw.append(load_w1(1, "raw_c", 1))
         wgs_rows.append(load_wgs(1))
         for s in range(2, 6):
             pages0.append(load_page0(s))
@@ -224,7 +226,7 @@ def tile_list_sewer_defect_recall_kernel(
             product_banks, turn_banks = 4 * (batch % 2), 4 * (1 - batch % 2)
             units = [(s, h) for s in slices for h in range(2)]
             neg_tanh = work.tile([P, len(units), HALF], F32, tag="tanh_root", align_bytes=64, name="neg_tanh")
-            scaled = {s: work.tile([P, S], F32, tag="aw%d" % (s % 2), align_bytes=64, name="scaled") for s in slices}
+            scaled = work.tile([P, 2, S], F32, tag="scaled", name="scaled")
             a_banks, back_banks = [], []
             for u, (s, h) in enumerate(units):
                 b_sb = work.tile([P, HALF], F32, tag="b_sb", bufs=2, name="b_sb")
@@ -238,7 +240,10 @@ def tile_list_sewer_defect_recall_kernel(
                 gap_sq = work.tile([P, HALF], F32, tag="gap_sq", bufs=4, name="gap_sq")
                 if on_vector:
                     nc.vector.tensor_tensor(b_sb[:], b[:], neg_tanh[:, u, :], ADD)
-                    nc.vector.tensor_tensor(gap_sq[:], b_sb[:], b_sb[:], MULT)
+                    if h == 0:
+                        nc.scalar.activation(gap_sq[:], b_sb[:], ACT.Square)
+                    else:
+                        nc.vector.tensor_tensor(gap_sq[:], b_sb[:], b_sb[:], MULT)
                 else:
                     gap = bank(turn_banks + u, "gap")
                     for c in range(4):
@@ -251,7 +256,7 @@ def tile_list_sewer_defect_recall_kernel(
             for u, (s, h) in enumerate(units):
                 g, t = divmod(s, PACK)
                 nc.vector.scalar_tensor_tensor(
-                    scaled[s][:, half(h)], a_banks[u][:], gains[:, g, t : t + 1], wgs_rows[t // 2][:, t % 2, half(h)], MULT, MULT
+                    scaled[:, s % 2, half(h)], a_banks[u][:], gains[:, g, t : t + 1], wgs_rows[t // 2][:, t % 2, half(h)], MULT, MULT
                 )
             root = work.tile([P, len(units), HALF], F32, tag="tanh_root", align_bytes=64, name="root")
             damp = {s: work.tile([P, S], F32, tag="damp", bufs=3, name="damp") for s in slices}
@@ -269,10 +274,10 @@ def tile_list_sewer_defect_recall_kernel(
                 if s == 0:
                     for h in range(2):
                         nc.vector.tensor_tensor(
-                            pages0[s][:].indirect(list2[:, list_half(h)]), damp[s][:, half(h)], scaled[s][:, half(h)], MULT
+                            pages0[s][:].indirect(list2[:, list_half(h)]), damp[s][:, half(h)], scaled[:, s % 2, half(h)], MULT
                         )
                 else:
-                    nc.vector.tensor_tensor(pages0[s][:].indirect(list2[:]), damp[s][:], scaled[s][:], MULT)
+                    nc.vector.tensor_tensor(pages0[s][:].indirect(list2[:]), damp[s][:], scaled[:, s % 2, :], MULT)
                 if s < PACK:
                     gather_first_pass(s)
                 else:

@@ -72,15 +72,12 @@ def tile_list_sewer_defect_recall_kernel(
 
         def load_page0(s):
             g, t = divmod(s, PACK)
-            tile = work.tile([P, T2], F32, tag="page0", bufs=6, name="page0_rows")
+            tile = work.tile([P, T2], F32, tag="page", bufs=8, name="page0_rows")
             nc.sync.dma_start(tile[:], page0[half(g), :].rearrange("(p t) c -> t p c", t=PACK)[t])
             return tile
 
         def load_page1(n):
-            if n < 4:
-                tile = work.tile([P, T2], F32, tag="page1", bufs=4, name="page1_rows")
-            else:
-                tile = work.tile([P, T2], F32, tag="page0", bufs=6, name="page1_rows")
+            tile = work.tile([P, T2], F32, tag="page", bufs=8, name="page1_rows")
             nc.sync.dma_start(tile[:], page1[n * P : (n + 1) * P, :])
             return tile
 
@@ -152,9 +149,8 @@ def tile_list_sewer_defect_recall_kernel(
         nc.vector.tensor_copy(v_codes[1][:], tab_w[:].indirect(list1[:, list_half(1)]))
         pages0.append(load_page0(1))
         wgs_rows.append(load_wgs(1))
-        for s in range(2, 6):
+        for s in range(2, SLICES):
             pages0.append(load_page0(s))
-        pages1 = [load_page1(n) for n in range(4)]
 
         w3_codes = [keep.tile([P, N], U32, align_bytes=64, name="w3_codes%d" % g) for g in range(PASSES)]
         w3_sc = [keep.tile([P, N], U8, align_bytes=64, name="w3_sc%d" % g) for g in range(PASSES)]
@@ -167,7 +163,7 @@ def tile_list_sewer_defect_recall_kernel(
             for b in range(0, width // 4, step):
                 nc.scalar.copy(dst[:, b : b + step], src[:, b : b + step])
 
-        picked_first = work.tile([P, PACK, M], BF16, tag="x0", align_bytes=64, name="picked_first")
+        picked_first = work.tile([P, PACK, M], F32, tag="x0", align_bytes=64, name="picked_first")
         picked_second = []
 
         def gather_first_pass(s):
@@ -175,7 +171,7 @@ def tile_list_sewer_defect_recall_kernel(
 
         def gather_second_pass(s, h):
             if s == PACK:
-                picked_second.append(work.tile([P, PACK, HALF], BF16, tag=("x10", "stage0")[h], align_bytes=64, name="picked_second"))
+                picked_second.append(work.tile([P, PACK, HALF], F32, tag=("x10", "stage0")[h], align_bytes=64, name="picked_second"))
             nc.vector.tensor_copy(picked_second[h][:, s - PACK, :], pages0[s][:].indirect(list3[:, list_half(h)]))
 
         def prepare_w3_and_first_pass():
@@ -286,19 +282,18 @@ def tile_list_sewer_defect_recall_kernel(
         stage_one(0, (0, 1))
         prepare_w1(1)
         deal_w2_scales(1)
-        pages0.append(load_page0(6))
-        pages0.append(load_page0(7))
         w3_raw = [load_w3(g) for g in range(PASSES)]
         stage_one(1, (2, 3))
+        pages1 = [load_page1(n) for n in range(4)]
         stage_one(2, (4, 5))
         wgo_rows = work.tile([P, M], F32, tag="wgs0", name="wgo_rows")
         nc.sync.dma_start(wgo_rows[:], wgo)
-        pages1.extend(load_page1(n) for n in range(4, OUT_SLICES))
         stage_one(3, (6, 7))
         prepare_w3_and_first_pass()
         prepare_x_second_pass(0)
         for s in range(PACK, SLICES):
             gather_second_pass(s, 1)
+        pages1.extend(load_page1(n) for n in range(4, OUT_SLICES))
 
         def scores(n, h, size):
             cols = slice(n * P, (n + 1) * P)

from contextlib import ExitStack

import concourse.mybir as mybir
from concourse.masks import make_identity

T, S, K, H, N, T2, M = 4096, 1024, 512, 1024, 768, 2048, 1024
FLOPS = 2 * (2 * K * H * S + H * N * M)

F32 = mybir.dt.float32
BF16 = mybir.dt.bfloat16
I32 = mybir.dt.int32
U32 = mybir.dt.uint32
U16 = mybir.dt.uint16
U8 = mybir.dt.uint8
FP8X4 = mybir.dt.float8_e4m3fn_x4
FP4X4 = mybir.dt.float4_e2m1fn_x4
ACT = mybir.ActivationFunctionType
MULT = mybir.AluOpType.mult
ADD = mybir.AluOpType.add

P = 128
PACK = 4
HALF = 512
LIST_HALF = HALF // 16
PASSES = H // (P * PACK)
SLICES = H // P
OUT_SLICES = N // P


def tile_list_sewer_defect_recall_kernel(
    tc, tab_words, tab_scales, offs, w1, w2_words, w2_scales, gain, page0, wgs, offs2, offs3, w3, page1, wgo, offs4, out
):
    nc = tc.nc
    with ExitStack() as ctx:
        keep = ctx.enter_context(tc.tile_pool(name="keep", bufs=1))
        work = ctx.enter_context(tc.tile_pool(name="work", bufs=1))
        psum = ctx.enter_context(tc.psum_pool(name="psum", bufs=1))

        def half(h):
            return slice(h * HALF, (h + 1) * HALF)

        def list_half(h):
            return slice(h * LIST_HALF, (h + 1) * LIST_HALF)

        def load_list(src, name):
            tile = keep.tile([P, S // 16], U16, name=name)
            nc.sync.dma_start(tile[:], src)
            return tile

        def load_scale_rows(queue, tile, src):
            for q in range(4):
                queue.dma_start(tile[32 * q : 32 * q + 4, :].bitcast(I32), src[0, 4 * q : 4 * q + 4, :].bitcast(I32))

        def load_w1(g, tag, parts):
            raw = work.tile([P, PACK, HALF], F32, tag=tag, align_bytes=64, name="w1_raw")
            rows = w1[:, half(g)].rearrange("(p j) c -> p j c", j=PACK)
            for j in range(0, PACK, PACK // parts):
                nc.sync.dma_start(raw[:, j : j + PACK // parts, :], rows[:, j : j + PACK // parts, :])
            return raw

        def load_w3(g):
            raw = work.tile([P, PACK, N], F32, tag=("raw_a", "raw_b")[g], align_bytes=64, name="w3_raw")
            nc.sync.dma_start(raw[:], w3[half(g), :].rearrange("(p j) c -> p j c", j=PACK))
            return raw

        def load_wgs(pair):
            tile = work.tile([P, 2, S], F32, tag="wgs%d" % pair, name="wgs_rows")
            rows = wgs.rearrange("(q t) j -> q t j", t=PACK)[:, 2 * pair : 2 * pair + 2, :]
            for q in range(4):
                nc.sync.dma_start(tile[32 * q : 32 * q + 32, :, :], rows)
            return tile

        def load_page0(s):
            g, t = divmod(s, PACK)
            tile = work.tile([P, T2], F32, tag="page", bufs=8, name="page0_rows")
            nc.sync.dma_start(tile[:], page0[half(g), :].rearrange("(p t) c -> t p c", t=PACK)[t])
            return tile

        def load_page1(n):
            tile = work.tile([P, T2], F32, tag="page", bufs=8, name="page1_rows")
            nc.sync.dma_start(tile[:], page1[n * P : (n + 1) * P, :])
            return tile

        tab_sc = work.tile([P, T], U8, tag="tabsc", align_bytes=64, name="tab_sc")
        nc.vector.memset(tab_sc[:].bitcast(I32), 0)
        w2_sc_raw = keep.tile([P, H], U8, name="w2_sc_raw")
        nc.vector.memset(w2_sc_raw[:].bitcast(I32), 0)
        ident = keep.tile([P, P], F32, name="ident")
        make_identity(nc, ident[:])

        list1 = load_list(offs, "list1")
        list2 = load_list(offs2, "list2")
        list3 = load_list(offs3, "list3")
        list4 = load_list(offs4, "list4")
        gains = keep.tile([P, PASSES, PACK], F32, name="gains")
        nc.sync.dma_start(gains[:], gain.rearrange("(g p t) -> p g t", g=PASSES, t=PACK))
        w2_raw = keep.tile([P, 2 * H], U8, name="w2_raw")
        nc.sync.dma_start(w2_raw[:].bitcast(I32), w2_words[0].bitcast(I32))
        w1_raw = [load_w1(0, "raw_a", 2)]
        load_scale_rows(nc.sync, tab_sc, tab_scales)
        tab_w = work.tile([P, T], U32, tag="raw_b", align_bytes=64, name="tab_w")
        nc.sync.dma_start(tab_w[:].bitcast(I32), tab_words[0].rearrange("p n t -> p (n t)").bitcast(I32))
        load_scale_rows(nc.sync, w2_sc_raw, w2_scales)
        w1_raw.append(load_w1(1, "raw_c", 1))
        wgs_rows = [load_wgs(0)]
        pages0 = [load_page0(0)]

        w1_codes = []
        w1_sc = [keep.tile([P, HALF], U8, align_bytes=64, name="w1_sc%d" % g) for g in range(PASSES)]
        w2_codes = [keep.tile([P, 2 * HALF], U8, align_bytes=64, name="w2_codes%d" % g) for g in range(PASSES)]
        w2_sc = []

        def staging(tag, width=PACK * HALF):
            return work.tile([P, width], BF16, tag=tag, align_bytes=64, name="staging")

        def prepare_w1(g):
            grouped = staging(("stage0", "raw_b")[g])
            dst = grouped[:].rearrange("p (t m j) -> p m t j", t=PACK, j=PACK)
            src = w1_raw[g][:].rearrange("p j (m t) -> p m t j", t=PACK)
            if g == 0:
                nc.scalar.copy(dst, src)
            else:
                for m in range(0, P, 32):
                    nc.gpsimd.tensor_scalar(dst[:, m : m + 32], src[:, m : m + 32], 1.0, 0.0, MULT, ADD)
            w1_codes.append(work.tile([P, HALF], U32, tag=("tabsc", "w1_second")[g], align_bytes=64, name="w1_codes"))
            nc.vector.quantize_mx(out=w1_codes[g][:].bitcast(FP8X4), scales=w1_sc[g][:], in_=grouped[:])

        def deal_w2_codes(g):
            nc.vector.tensor_copy(
                w2_codes[g][:].rearrange("p (t m b) -> p t m b", t=PACK, b=2),
                w2_raw[:, 2 * HALF * g : 2 * HALF * (g + 1)].rearrange("p (m t b) -> p t m b", t=PACK, b=2),
            )

        def deal_w2_scales(g):
            w2_sc.append(work.tile([P, HALF], U8, tag=("w2_first", "raw_c")[g], align_bytes=64, name="w2_sc"))
            nc.vector.tensor_copy(
                w2_sc[g][:].rearrange("p (t m) -> p t m", t=PACK),
                w2_sc_raw[:, half(g)].rearrange("p (m t) -> p t m", t=PACK),
            )

        v_sc = keep.tile([P, S], U8, align_bytes=64, name="v_sc")
        v_codes = [keep.tile([P, HALF], U32, align_bytes=64, name="v_codes%d" % h) for h in range(2)]
        for g in range(PASSES):
            deal_w2_codes(g)
        nc.vector.tensor_copy(v_sc[:], tab_sc[:].indirect(list1[:]))
        prepare_w1(0)
        nc.vector.tensor_copy(v_codes[0][:], tab_w[:].indirect(list1[:, list_half(0)]))
        deal_w2_scales(0)
        nc.vector.tensor_copy(v_codes[1][:], tab_w[:].indirect(list1[:, list_half(1)]))
        pages0.append(load_page0(1))
        wgs_rows.append(load_wgs(1))
        for s in range(2, SLICES):
            pages0.append(load_page0(s))

        w3_codes = [keep.tile([P, N], U32, align_bytes=64, name="w3_codes%d" % g) for g in range(PASSES)]
        w3_sc = [keep.tile([P, N], U8, align_bytes=64, name="w3_sc%d" % g) for g in range(PASSES)]
        x_codes = [keep.tile([P, M], U32, align_bytes=64, name="x_codes%d" % g) for g in range(PASSES)]
        x_sc = [keep.tile([P, M], U8, align_bytes=64, name="x_sc%d" % g) for g in range(PASSES)]

        def interleave(grouped, planes, c0, width, step=64):
            dst = grouped.rearrange("p (c i t) -> p c t i", i=4, t=PACK)
            src = planes[:, :, c0 : c0 + width].rearrange("p t (c i) -> p c t i", i=4)
            for b in range(0, width // 4, step):
                nc.scalar.copy(dst[:, b : b + step], src[:, b : b + step])

        picked_first = work.tile([P, PACK, M], F32, tag="x0", align_bytes=64, name="picked_first")
        picked_second = []

        def gather_first_pass(s):
            nc.vector.tensor_copy(picked_first[:, s, :], pages0[s][:].indirect(list3[:]))

        def gather_second_pass(s, h):
            if s == PACK:
                picked_second.append(work.tile([P, PACK, HALF], F32, tag=("x10", "stage0")[h], align_bytes=64, name="picked_second"))
            nc.vector.tensor_copy(picked_second[h][:, s - PACK, :], pages0[s][:].indirect(list3[:, list_half(h)]))

        def prepare_w3_and_first_pass():
            grouped = staging("tanh_root", PACK * (PASSES * N + M))
            for g in range(PASSES):
                interleave(grouped[:, PACK * N * g : PACK * N * (g + 1)], w3_raw[g], 0, N)
            x_at = PACK * N * PASSES
            interleave(grouped[:, x_at:], picked_first, 0, M)
            for g in range(PASSES):
                for c0, c1 in ((0, HALF), (HALF, N)):
                    nc.vector.quantize_mx(
                        out=w3_codes[g][:, c0:c1].bitcast(FP8X4),
                        scales=w3_sc[g][:, c0:c1],
                        in_=grouped[:, PACK * (N * g + c0) : PACK * (N * g + c1)],
                    )
            nc.vector.quantize_mx(out=x_codes[0][:].bitcast(FP8X4), scales=x_sc[0][:], in_=grouped[:, x_at:])

        def prepare_x_second_pass(h):
            grouped = staging(("stage0", "x10")[h])
            interleave(grouped[:], picked_second[h], 0, HALF, 32)
            nc.vector.quantize_mx(out=x_codes[1][:, half(h)].bitcast(FP8X4), scales=x_sc[1][:, half(h)], in_=grouped[:])

        def bank(index, name):
            return psum.tile([P, HALF], F32, tag="bank%d" % index, name=name)

        def features(index, s, h, neg_tanh):
            g, t = divmod(s, PACK)
            cols = slice(t * P, (t + 1) * P)
            a = bank(index, "a")
            nc.tensor.matmul_mx(
                out=a[:], lhsT=w1_codes[g][:, cols].bitcast(FP8X4), lhsT_scale=w1_sc[g][:, cols],
                rhs=v_codes[h][:].bitcast(FP8X4), rhs_scale=v_sc[:, half(h)], start=True, stop=True,
            )
            nc.scalar.activation(neg_tanh, a[:], ACT.Tanh, scale=-1.0)
            return a

        def codes(index, s, h):
            g, t = divmod(s, PACK)
            b = bank(index, "b")
            nc.tensor.matmul_mx(
                out=b[:], lhsT=w2_codes[g][:, 2 * t * P : 2 * (t + 1) * P].bitcast(FP4X4), lhsT_scale=w2_sc[g][:, t * P : (t + 1) * P],
                rhs=v_codes[h][:].bitcast(FP8X4), rhs_scale=v_sc[:, half(h)], start=True, stop=True,
            )
            return b

        def stage_one(batch, slices):
            on_vector = batch == 0
            product_banks, turn_banks = 4 * (batch % 2), 4 * (1 - batch % 2)
            units = [(s, h) for s in slices for h in range(2)]
            neg_tanh = work.tile([P, len(units), HALF], F32, tag="tanh_root", align_bytes=64, name="neg_tanh")
            scaled = work.tile([P, 2, S], F32, tag="scaled", name="scaled")
            a_banks, back_banks = [], []
            for u, (s, h) in enumerate(units):
                b_sb = work.tile([P, HALF], F32, tag="b_sb", bufs=2, name="b_sb")
                if on_vector:
                    a = features(product_banks + u, s, h, neg_tanh[:, u, :])
                    b = codes(turn_banks + u, s, h)
                else:
                    b = codes(product_banks + u, s, h)
                    nc.scalar.copy(b_sb[:], b[:])
                    a = features(product_banks + u, s, h, neg_tanh[:, u, :])
                gap_sq = work.tile([P, HALF], F32, tag="gap_sq", bufs=4, name="gap_sq")
                if on_vector:
                    nc.vector.tensor_tensor(b_sb[:], b[:], neg_tanh[:, u, :], ADD)
                    if h == 0:
                        nc.scalar.activation(gap_sq[:], b_sb[:], ACT.Square)
                    else:
                        nc.vector.tensor_tensor(gap_sq[:], b_sb[:], b_sb[:], MULT)
                else:
                    gap = bank(turn_banks + u, "gap")
                    for c in range(4):
                        blk = slice(c * P, (c + 1) * P)
                        nc.tensor.matmul(gap[:, blk], neg_tanh[:, u, blk], ident[:], start=True, stop=False, is_transpose=True)
                        nc.tensor.matmul(gap[:, blk], b_sb[:, blk], ident[:], start=False, stop=True, is_transpose=True)
                    nc.scalar.activation(gap_sq[:], gap[:], ACT.Square)
                a_banks.append(a)
                back_banks.append(gap_sq)
            for u, (s, h) in enumerate(units):
                g, t = divmod(s, PACK)
                nc.vector.scalar_tensor_tensor(
                    scaled[:, s % 2, half(h)], a_banks[u][:], gains[:, g, t : t + 1], wgs_rows[t // 2][:, t % 2, half(h)], MULT, MULT
                )
            root = work.tile([P, len(units), HALF], F32, tag="tanh_root", align_bytes=64, name="root")
            damp = {s: work.tile([P, S], F32, tag="damp", bufs=3, name="damp") for s in slices}
            for u, (s, h) in enumerate(units):
                if on_vector:
                    back = back_banks[u]
                else:
                    back = bank(turn_banks + u, "back")
                    for c in range(4):
                        blk = slice(c * P, (c + 1) * P)
                        nc.tensor.transpose(back[:, blk], back_banks[u][:, blk], ident[:])
                nc.scalar.activation(root[:, u, :], back[:], ACT.Abs_reciprocal_sqrt, bias=1.0)
                nc.scalar.activation(damp[s][:, half(h)], root[:, u, :], ACT.Square)
            for s in slices:
                if s == 0:
                    for h in range(2):
                        nc.vector.tensor_tensor(
                            pages0[s][:].indirect(list2[:, list_half(h)]), damp[s][:, half(h)], scaled[:, s % 2, half(h)], MULT
                        )
                else:
                    nc.vector.tensor_tensor(pages0[s][:].indirect(list2[:]), damp[s][:], scaled[:, s % 2, :], MULT)
                if s < PACK:
                    gather_first_pass(s)
                else:
                    gather_second_pass(s, 0)

        stage_one(0, (0, 1))
        prepare_w1(1)
        deal_w2_scales(1)
        w3_raw = [load_w3(g) for g in range(PASSES)]
        stage_one(1, (2, 3))
        pages1 = [load_page1(n) for n in range(4)]
        stage_one(2, (4, 5))
        wgo_rows = work.tile([P, M], F32, tag="wgs0", name="wgo_rows")
        nc.sync.dma_start(wgo_rows[:], wgo)
        stage_one(3, (6, 7))
        prepare_w3_and_first_pass()
        prepare_x_second_pass(0)
        for s in range(PACK, SLICES):
            gather_second_pass(s, 1)
        pages1.extend(load_page1(n) for n in range(4, OUT_SLICES))

        def scores(n, h, size):
            cols = slice(n * P, (n + 1) * P)
            y = bank((2 * n + h) % 8, "y")
            for g in range(PASSES):
                nc.tensor.matmul_mx(
                    out=y[:], lhsT=w3_codes[g][:, cols].bitcast(FP8X4), lhsT_scale=w3_sc[g][:, cols],
                    rhs=x_codes[g][:, half(h)].bitcast(FP8X4), rhs_scale=x_sc[g][:, half(h)], start=(g == 0), stop=(g == PASSES - 1),
                )
            nc.scalar.activation(size, y[:], ACT.Abs)

        def store(n):
            nc.sync.dma_start(out[n * P : (n + 1) * P, :], pages1[n][:])

        def put_half(n, h):
            size = work.tile([P, HALF], F32, tag="gap_sq", bufs=4, name="size")
            scores(n, h, size[:])
            nc.vector.tensor_tensor(pages1[n][:].indirect(list4[:, list_half(h)]), size[:], wgo_rows[:, half(h)], MULT)

        def put_whole(n):
            size = work.tile([P, M], F32, tag="damp", bufs=3, name="size")
            for h in range(2):
                scores(n, h, size[:, half(h)])
            nc.vector.tensor_tensor(pages1[n][:].indirect(list4[:]), size[:], wgo_rows[:], MULT)

        put_half(0, 0)
        prepare_x_second_pass(1)
        put_half(1, 0)
        put_half(2, 0)
        for n in range(3):
            put_half(n, 1)
            store(n)
        for n in range(3, OUT_SLICES):
            put_whole(n)
            store(n)
